import numpy as np
import ml_dtypes


def mxq(x, axis, fmt="e4m3"):
    dtype, down = {"e4m3": (ml_dtypes.float8_e4m3fn, 7), "e5m2": (ml_dtypes.float8_e5m2, 14)}[fmt]
    v = np.moveaxis(np.asarray(x, np.float32).astype(ml_dtypes.bfloat16).astype(np.float64), axis, -1)
    blocks = v.reshape(v.shape[:-1] + (-1, 32))
    amax = np.abs(blocks).max(-1, keepdims=True)
    byte = np.maximum(np.where(amax > 0, np.frexp(amax)[1] - 1 + 127, 0) - down, 1)
    scale = np.exp2(byte - 127.0)
    codes = (blocks / scale).astype(np.float32).astype(dtype).astype(np.float64)
    return np.moveaxis((codes * scale).reshape(v.shape), -1, axis)


WIDE = False


def mx_kscale(k):
    if not WIDE:
        return np.ones(k)
    levels = np.array([10, -10, 5, -5, 0])
    if k % 512:
        return np.exp2(np.random.permutation(np.resize(levels, k // 32))).repeat(32)
    a = np.empty((k // 512, 16))
    for p in range(k // 512):
        a[p, :8] = np.random.permutation(np.resize(levels, 8))
        for g in range(8):
            far = levels[np.abs(levels - a[p, g]) >= 10]
            a[p, g + 8] = far[np.random.randint(len(far))]
    return np.exp2(a.ravel()).repeat(32)


def f64(x):
    return np.asarray(x).astype(np.float64)


def striped(idx):
    return np.tile(idx.reshape(-1, 16).T, (8, 1)).astype(np.uint16)


def unstriped(offs):
    return offs[:16].T.reshape(-1).astype(np.int64)


E2M1 = np.array([0.0, 0.5, 1.0, 1.5, 2.0, 3.0, 4.0, 6.0, -0.0, -0.5, -1.0, -1.5, -2.0, -3.0, -4.0, -6.0])


def pack_weight(w, fmt):
    k, n = w.shape
    w = f64(np.asarray(w, np.float32).astype(ml_dtypes.bfloat16)).reshape(k // 32, 32, n)
    amax = np.abs(w).max(1)
    if fmt == "e4m3":
        byte = np.frexp(amax)[1] - 1 + 127 - 7
    else:
        mant, ex = np.frexp(amax / 6.0)
        byte = np.where(mant > 0.5, ex, ex - 1) + 127
    byte = np.clip(np.where(amax > 0, byte, 1), 1, 254)
    scaled = (w * np.exp2(127.0 - byte)[:, None, :]).reshape(k, n).astype(np.float32)
    by_word = np.ascontiguousarray(scaled.reshape(k // 512, 128, 4, n).transpose(0, 1, 3, 2))
    if fmt == "e4m3":
        words = by_word.astype(ml_dtypes.float8_e4m3fn).view(np.uint8)
    else:
        c = by_word.astype(ml_dtypes.float4_e2m1fn).view(np.uint8) & 0xF
        words = (c[..., 0::2] | (c[..., 1::2] << 4)).reshape(k // 512, 128, 2 * n)
    return np.ascontiguousarray(words), np.ascontiguousarray(byte.astype(np.uint8).reshape(k // 512, 16, n))


def unpack_weight(words, scales, fmt):
    g, _, n = scales.shape
    words = np.ascontiguousarray(words).reshape(g, 128, n, -1)
    if fmt == "e4m3":
        vals = words.view(ml_dtypes.float8_e4m3fn).astype(np.float64)
    else:
        nib = np.empty((g, 128, n, 4), np.uint8)
        nib[..., 0::2] = words & 0xF
        nib[..., 1::2] = words >> 4
        vals = E2M1[nib]
    vals = vals * np.repeat(np.exp2(scales.astype(np.float64) - 127.0), 8, axis=1)[..., None]
    return vals.transpose(0, 1, 3, 2).reshape(g * 512, n)


def gelu(v):
    return 0.5 * v * (1.0 + np.tanh(np.sqrt(2.0 / np.pi) * (v + 0.044715 * v**3)))


K, T, E, C, H, N = 1024, 640, 4, 128, 1024, 256


def by_expert(wq, xq):
    return np.concatenate([wq[e].T @ xq[:, e * C:(e + 1) * C] for e in range(E)], axis=1)


def setup_inputs():
    n = np.random.standard_normal
    s = mx_kscale(K)[:, None]
    u = mx_kscale(H)
    x = pack_weight(n((K, T)) * s, "e4m3")
    return {
        "x_words": x[0],
        "x_scales": x[1],
        "w1": (n((E + 1, K, H)) / np.sqrt(K) / s[None] * u[None, None, :]).astype(np.float32),
        "w2": (n((E + 1, H, N)) / np.sqrt(H) / u[None, :, None]).astype(np.float32),
        "gate": np.tile(np.random.uniform(0.2, 1.0, E * C), (N, 1)).astype(np.float32),
        "offs": striped(np.random.permutation(T)[:E * C]),
    }


def reference(x_words, x_scales, w1, w2, gate, offs):
    idx = unstriped(offs)
    w1q, w2q = mxq(f64(w1), 1, "e4m3"), mxq(f64(w2), 1, "e4m3")
    xs = unpack_weight(x_words, x_scales, "e4m3")
    hs = gelu(w1q[E].T @ xs)
    ys = w2q[E].T @ mxq(hs, 0, "e4m3")
    xq = unpack_weight(x_words, x_scales, "e4m3")[:, idx]
    h = gelu(by_expert(w1q, xq))
    y = by_expert(w2q, mxq(h, 0, "e4m3"))
    out = ys
    out[:, idx] += f64(gate) * y
    return out

@@ -1,0 +1,218 @@
+from contextlib import ExitStack
+
+import concourse.mybir as mybir
+
+K, T, E, C, H, N = 1024, 640, 4, 128, 1024, 256
+S = E * C
+FLOPS = 2 * (S + T) * (K * H + H * N)
+
+F32 = mybir.dt.float32
+BF16 = mybir.dt.bfloat16
+I32 = mybir.dt.int32
+U32 = mybir.dt.uint32
+U16 = mybir.dt.uint16
+U8 = mybir.dt.uint8
+FP8X4 = mybir.dt.float8_e4m3fn_x4
+GELU = mybir.ActivationFunctionType.Gelu_apprx_tanh
+MULT = mybir.AluOpType.mult
+ADD = mybir.AluOpType.add
+
+P = 128
+PACK = 4
+KP = P * PACK
+PASSES = 2
+SHARED = E
+
+
+def tile_moe_shr_mlp_gelu_kernel(tc, x_words, x_scales, w1, w2, gate, offs, out):
+    nc = tc.nc
+    with ExitStack() as ctx:
+        keep = ctx.enter_context(tc.tile_pool(name="keep", bufs=1))
+        raws = ctx.enter_context(tc.tile_pool(name="raws", bufs=8))
+        stage = ctx.enter_context(tc.tile_pool(name="stage", bufs=4))
+        codes = ctx.enter_context(tc.tile_pool(name="codes", bufs=6))
+        two = ctx.enter_context(tc.tile_pool(name="two", bufs=2))
+        psum = ctx.enter_context(tc.psum_pool(name="psum", bufs=4))
+
+        offsets = keep.tile([P, S // 16], U16, name="offsets")
+        xw = keep.tile([P, PASSES * T], U32, name="xw", align_bytes=64)
+        xs = keep.tile([P, T], U8, name="xs", align_bytes=64)
+        gw = keep.tile([P, PASSES * S], U32, name="gw", align_bytes=64)
+        gs = keep.tile([P, S], U8, name="gs", align_bytes=64)
+        gate_sb = keep.tile([P, S], F32, name="gate_sb")
+        routed = [keep.tile([P, T], F32, name="routed%d" % h) for h in range(2)]
+
+        nc.vector.memset(xs[:].bitcast(I32), 0)
+        nc.sync.dma_start(
+            out=xw[:].bitcast(I32).rearrange("p (o t) -> p o t", o=PASSES),
+            in_=x_words.rearrange("o p t r -> p o (t r)").bitcast(I32),
+        )
+        nc.sync.dma_start(offsets[:], offs)
+        for q in range(4):
+            nc.sync.dma_start(
+                out=xs[32 * q : 32 * q + 8, :].bitcast(I32),
+                in_=x_scales[:, 4 * q : 4 * q + 4, :].bitcast(I32),
+            )
+        for h in range(2):
+            nc.vector.memset(routed[h][:], 0.0)
+        half = S // 2
+        for a in range(2):
+            lst = offsets[:, a * half // 16 : (a + 1) * half // 16]
+            for o in range(PASSES):
+                nc.vector.tensor_copy(gw[:, o * S + a * half : o * S + (a + 1) * half], xw[:, o * T : (o + 1) * T].indirect(lst))
+            nc.vector.tensor_copy(gs[:, a * half : (a + 1) * half], xs[:].indirect(lst))
+
+        def copy_on(engine, dst, src):
+            if engine == "s":
+                nc.scalar.copy(dst, src)
+            else:
+                nc.vector.tensor_copy(dst, src)
+
+        def quantise(src, width, tag, pool):
+            cw = pool.tile([P, width], U32, name=tag + "_w", align_bytes=64)
+            cs = pool.tile([P, width], U8, name=tag + "_s", align_bytes=64)
+            nc.vector.quantize_mx(out=cw[:].bitcast(FP8X4), scales=cs[:], in_=src)
+            return cw, cs
+
+        def cast_w1(raw, engine):
+            b = stage.tile([P, PACK * KP], BF16, name="w1b", align_bytes=64)
+            dst = b[:].rearrange("p (t m j) -> p m j t", t=PACK, j=PACK)
+            src = raw.rearrange("p j (m t) -> p m j t", t=PACK)
+            parts = 2 if engine == "s" else 1
+            for a in range(parts):
+                ms = slice(a * P // parts, (a + 1) * P // parts)
+                copy_on(engine, dst[:, ms], src[:, ms])
+            return b
+
+        def load_w1(e, o, split):
+            tag, pool = ("w1s%d" % o, two) if e == SHARED else ("w1q", codes)
+            rows = w1[e, o * KP : (o + 1) * KP, :].rearrange("(p j) c -> p j c", j=PACK)
+            if not split:
+                raw = raws.tile([P, PACK, H], F32, name="raw")
+                nc.sync.dma_start(out=raw[:], in_=rows)
+                views = [raw[:, :, g * KP : (g + 1) * KP] for g in range(PASSES)]
+            else:
+                views = []
+                for g in range(PASSES):
+                    raw = raws.tile([P, PACK, KP], F32, name="raw")
+                    nc.sync.dma_start(out=raw[:], in_=rows[:, :, g * KP : (g + 1) * KP])
+                    views.append(raw[:])
+            b0 = cast_w1(views[0], "s")
+            b1 = cast_w1(views[1], "v")
+            if split:
+                q0 = quantise(b0[:], KP, tag, pool)
+                q1 = quantise(b1[:], KP, tag, pool)
+            else:
+                q1 = quantise(b1[:], KP, tag, pool)
+                q0 = quantise(b0[:], KP, tag, pool)
+            return [q0, q1]
+
+        def cast_w2(raw, engine, width):
+            b = stage.tile([P, PACK * width], BF16, name="w2b", align_bytes=64)
+            copy_on(engine, b[:].rearrange("p (c i j) -> p c j i", i=4, j=PACK), raw.rearrange("p j (c i) -> p c j i", i=4))
+            return b
+
+        def load_w2(e):
+            raw = raws.tile([P, PASSES, PACK, N], F32, name="raw")
+            nc.sync.dma_start(out=raw[:].rearrange("p o j n -> p o (j n)"), in_=w2[e].rearrange("(o p j) n -> p o (j n)", o=PASSES, j=PACK))
+            bs = [cast_w2(raw[:, o], "sv"[o], N) for o in range(PASSES)]
+            q1 = quantise(bs[1][:], N, "w2q", codes)
+            q0 = quantise(bs[0][:], N, "w2q", codes)
+            return [q0, q1]
+
+        def layer1_block(w1q, g, words, scales, width, c0, hb, tag):
+            bank = psum.tile([P, PACK, C], F32, name=tag)
+            for t in range(PACK):
+                for o in range(PASSES):
+                    cw, cs = w1q[o][g]
+                    nc.tensor.matmul_mx(
+                        out=bank[:, t, :],
+                        lhsT=cw[:, t * P : (t + 1) * P].bitcast(FP8X4),
+                        lhsT_scale=cs[:, t * P : (t + 1) * P],
+                        rhs=words[:, o * width + c0 : o * width + c0 + C].bitcast(FP8X4),
+                        rhs_scale=scales[4 * o : P, c0 : c0 + C],
+                        start=(o == 0),
+                        stop=(o == PASSES - 1),
+                    )
+            nc.scalar.activation(hb.rearrange("p (n t) -> p n t", t=PACK), bank[:].rearrange("p t n -> p n t"), GELU)
+
+        def layer1_routed(e, w1q):
+            hq = {}
+            for g in ((0, 1) if e == E - 1 else (1, 0)):
+                hb = stage.tile([P, PACK * C], BF16, name="hb", align_bytes=64)
+                layer1_block(w1q, g, gw, gs, S, e * C, hb[:], "bank")
+                hq[g] = quantise(hb[:], C, "hq", codes)
+            return hq
+
+        def layer2_routed(e, w2q, hq):
+            bank = psum.tile([P, 2, C], F32, name="bank")
+            for h in range(2):
+                for g in range(PASSES):
+                    nc.tensor.matmul_mx(
+                        out=bank[:, h, :],
+                        lhsT=w2q[g][0][:, h * P : (h + 1) * P].bitcast(FP8X4),
+                        lhsT_scale=w2q[g][1][:, h * P : (h + 1) * P],
+                        rhs=hq[g][0][:].bitcast(FP8X4),
+                        rhs_scale=hq[g][1][:],
+                        start=(g == 0),
+                        stop=(g == PASSES - 1),
+                    )
+            y = stage.tile([P, 2, C], F32, name="y")
+            nc.scalar.copy(y[:], bank[:])
+            lst = offsets[:, e * C // 16 : (e + 1) * C // 16]
+            for h in range(2):
+                nc.vector.tensor_tensor(routed[h][:].indirect(lst), y[:, h, :], gate_sb[:, e * C : (e + 1) * C], MULT)
+
+        w1q = [load_w1(SHARED, o, False) for o in range(PASSES)]
+        nc.sync.dma_start(out=gate_sb[:], in_=gate[0:P, :])
+        hs_w = [keep.tile([P, T], U32, name="hs_w%d" % g, align_bytes=64) for g in range(PASSES)]
+        hs_s = [keep.tile([P, T], U8, name="hs_s%d" % g, align_bytes=64) for g in range(PASSES)]
+        w1q_shared = w1q
+
+        def layer1_shared(g):
+            hb = keep.tile([P, PACK * T], BF16, name="hsb%d" % g, align_bytes=64)
+            for b in range(T // C):
+                layer1_block(w1q_shared, g, xw, xs, T, b * C, hb[:, b * PACK * C : (b + 1) * PACK * C], "bank_s")
+            for c0, c1 in ((0, 512), (512, T)):
+                nc.vector.quantize_mx(out=hs_w[g][:, c0:c1].bitcast(FP8X4), scales=hs_s[g][:, c0:c1], in_=hb[:, PACK * c0 : PACK * c1])
+
+        for e in range(E):
+            w1q = [load_w1(e, o, e == E - 1 and o == PASSES - 1) for o in range(PASSES)]
+            hq = layer1_routed(e, w1q)
+            w2q = load_w2(e)
+            layer2_routed(e, w2q, hq)
+            if e in [1, 2]:
+                layer1_shared([1, 2].index(e))
+
+        spans = ((0, 512), (512, T))
+        banks = [[psum.tile([P, c1 - c0], F32, name="bank_s") for c0, c1 in spans] for h in range(2)]
+
+        def shared_pass(g, h, cw, cs):
+            for i, (c0, c1) in enumerate(spans):
+                nc.tensor.matmul_mx(
+                    out=banks[h][i][:],
+                    lhsT=cw.bitcast(FP8X4),
+                    lhsT_scale=cs,
+                    rhs=hs_w[g][:, c0:c1].bitcast(FP8X4),
+                    rhs_scale=hs_s[g][:, c0:c1],
+                    start=(g == 0),
+                    stop=(g == PASSES - 1),
+                )
+
+        for g in range(PASSES):
+            raw = raws.tile([P, PACK, N], F32, name="raw")
+            nc.sync.dma_start(out=raw[:], in_=w2[SHARED, g * KP : (g + 1) * KP, :].rearrange("(p j) n -> p j n", j=PACK))
+            if g == 0:
+                cw, cs = quantise(cast_w2(raw[:], "s", N)[:], N, "w2q", codes)
+                for h in range(2):
+                    shared_pass(g, h, cw[:, h * P : (h + 1) * P], cs[:, h * P : (h + 1) * P])
+            else:
+                bs = [cast_w2(raw[:, :, h * P : (h + 1) * P], "vs"[h], P) for h in range(2)]
+                for h in range(2):
+                    cw, cs = quantise(bs[h][:], P, "w2q", codes)
+                    shared_pass(g, h, cw[:], cs[:])
+        for h in range(2):
+            res = keep.tile([P, T], F32, name="res%d" % h)
+            for i, (c0, c1) in enumerate(spans):
+                nc.vector.tensor_tensor(res[:, c0:c1], banks[h][i][:], routed[h][:, c0:c1], ADD)
+            nc.sync.dma_start(out=out[h * P : (h + 1) * P, :], in_=res[:])

@@ -22,6 +22,7 @@ PACK = 4
 KP = P * PACK
 PASSES = 2
 SHARED = E
+ORDER = ["a40sssv","a41sssv","g0","a00sssv","a01svvv","h0","b0sv","y0","a10sssv","a11svvv","h1","b1sv","y1","s0","s1","a20sssv","a21svvv","h2","a30svvv","A31svsv","h3","b2sv","y2","b3sv","y3","c0s","c1ss"]
 
 
 def tile_moe_shr_mlp_gelu_kernel(tc, x_words, x_scales, w1, w2, gate, offs, out):
@@ -74,51 +75,41 @@ def tile_moe_shr_mlp_gelu_kernel(tc, x_words, x_scales, w1, w2, gate, offs, out)
             nc.vector.quantize_mx(out=cw[:].bitcast(FP8X4), scales=cs[:], in_=src)
             return cw, cs
 
-        def cast_w1(raw, engine):
+        def cast_w1(raw, engines):
             b = stage.tile([P, PACK * KP], BF16, name="w1b", align_bytes=64)
-            dst = b[:].rearrange("p (t m j) -> p m j t", t=PACK, j=PACK)
-            src = raw.rearrange("p j (m t) -> p m j t", t=PACK)
-            parts = 2 if engine == "s" else 1
-            for a in range(parts):
-                ms = slice(a * P // parts, (a + 1) * P // parts)
-                copy_on(engine, dst[:, ms], src[:, ms])
+            dst = b[:].rearrange("p (u t m j) -> p u m j t", u=2, t=2, j=PACK)
+            src = raw.rearrange("p j (m u t) -> p u m j t", u=2, t=2)
+            for u in range(2):
+                copy_on(engines[u], dst[:, u], src[:, u])
             return b
 
-        def load_w1(e, o, split):
+        def load_w1(e, o, engines, split):
             tag, pool = ("w1s%d" % o, two) if e == SHARED else ("w1q", codes)
             rows = w1[e, o * KP : (o + 1) * KP, :].rearrange("(p j) c -> p j c", j=PACK)
+            q = {}
             if not split:
                 raw = raws.tile([P, PACK, H], F32, name="raw")
                 nc.sync.dma_start(out=raw[:], in_=rows)
-                views = [raw[:, :, g * KP : (g + 1) * KP] for g in range(PASSES)]
+                b = {g: cast_w1(raw[:, :, g * KP : (g + 1) * KP], engines[2 * g : 2 * g + 2]) for g in (1, 0)}
+                for g in (1, 0):
+                    q[g] = quantise(b[g][:], KP, tag, pool)
             else:
-                views = []
-                for g in range(PASSES):
+                for g in (1, 0):
                     raw = raws.tile([P, PACK, KP], F32, name="raw")
                     nc.sync.dma_start(out=raw[:], in_=rows[:, :, g * KP : (g + 1) * KP])
-                    views.append(raw[:])
-            b0 = cast_w1(views[0], "s")
-            b1 = cast_w1(views[1], "v")
-            if split:
-                q0 = quantise(b0[:], KP, tag, pool)
-                q1 = quantise(b1[:], KP, tag, pool)
-            else:
-                q1 = quantise(b1[:], KP, tag, pool)
-                q0 = quantise(b0[:], KP, tag, pool)
-            return [q0, q1]
+                    q[g] = quantise(cast_w1(raw[:], engines[2 * g : 2 * g + 2])[:], KP, tag, pool)
+            return q
 
         def cast_w2(raw, engine, width):
             b = stage.tile([P, PACK * width], BF16, name="w2b", align_bytes=64)
-            copy_on(engine, b[:].rearrange("p (c i j) -> p c j i", i=4, j=PACK), raw.rearrange("p j (c i) -> p c j i", i=4))
+            copy_on(engine, b[:].rearrange("p (c i j) -> p c j i", i=2, j=PACK), raw.rearrange("p j (c i) -> p c j i", i=2))
             return b
 
-        def load_w2(e):
+        def load_w2(e, engines):
             raw = raws.tile([P, PASSES, PACK, N], F32, name="raw")
             nc.sync.dma_start(out=raw[:].rearrange("p o j n -> p o (j n)"), in_=w2[e].rearrange("(o p j) n -> p o (j n)", o=PASSES, j=PACK))
-            bs = [cast_w2(raw[:, o], "sv"[o], N) for o in range(PASSES)]
-            q1 = quantise(bs[1][:], N, "w2q", codes)
-            q0 = quantise(bs[0][:], N, "w2q", codes)
-            return [q0, q1]
+            b = {o: cast_w2(raw[:, o], engines[o], N) for o in (1, 0)}
+            return {o: quantise(b[o][:], N, "w2q", codes) for o in (1, 0)}
 
         def layer1_block(w1q, g, words, scales, width, c0, hb, tag):
             bank = psum.tile([P, PACK, C], F32, name=tag)
@@ -138,7 +129,7 @@ def tile_moe_shr_mlp_gelu_kernel(tc, x_words, x_scales, w1, w2, gate, offs, out)
 
         def layer1_routed(e, w1q):
             hq = {}
-            for g in ((0, 1) if e == E - 1 else (1, 0)):
+            for g in (1, 0):
                 hb = stage.tile([P, PACK * C], BF16, name="hb", align_bytes=64)
                 layer1_block(w1q, g, gw, gs, S, e * C, hb[:], "bank")
                 hq[g] = quantise(hb[:], C, "hq", codes)
@@ -147,72 +138,83 @@ def tile_moe_shr_mlp_gelu_kernel(tc, x_words, x_scales, w1, w2, gate, offs, out)
         def layer2_routed(e, w2q, hq):
             bank = psum.tile([P, 2, C], F32, name="bank")
             for h in range(2):
-                for g in range(PASSES):
+                for g in (1, 0):
                     nc.tensor.matmul_mx(
                         out=bank[:, h, :],
                         lhsT=w2q[g][0][:, h * P : (h + 1) * P].bitcast(FP8X4),
                         lhsT_scale=w2q[g][1][:, h * P : (h + 1) * P],
                         rhs=hq[g][0][:].bitcast(FP8X4),
                         rhs_scale=hq[g][1][:],
-                        start=(g == 0),
-                        stop=(g == PASSES - 1),
+                        start=(g == 1),
+                        stop=(g == 0),
                     )
             y = stage.tile([P, 2, C], F32, name="y")
-            nc.scalar.copy(y[:], bank[:])
+            copy_on("s", y[:], bank[:])
             lst = offsets[:, e * C // 16 : (e + 1) * C // 16]
             for h in range(2):
                 nc.vector.tensor_tensor(routed[h][:].indirect(lst), y[:, h, :], gate_sb[:, e * C : (e + 1) * C], MULT)
 
-        w1q = [load_w1(SHARED, o, False) for o in range(PASSES)]
-        nc.sync.dma_start(out=gate_sb[:], in_=gate[0:P, :])
         hs_w = [keep.tile([P, T], U32, name="hs_w%d" % g, align_bytes=64) for g in range(PASSES)]
         hs_s = [keep.tile([P, T], U8, name="hs_s%d" % g, align_bytes=64) for g in range(PASSES)]
-        w1q_shared = w1q
 
-        def layer1_shared(g):
+        def layer1_shared(g, w1q):
             hb = keep.tile([P, PACK * T], BF16, name="hsb%d" % g, align_bytes=64)
             for b in range(T // C):
-                layer1_block(w1q_shared, g, xw, xs, T, b * C, hb[:, b * PACK * C : (b + 1) * PACK * C], "bank_s")
+                layer1_block(w1q, g, xw, xs, T, b * C, hb[:, b * PACK * C : (b + 1) * PACK * C], "bank_s")
             for c0, c1 in ((0, 512), (512, T)):
                 nc.vector.quantize_mx(out=hs_w[g][:, c0:c1].bitcast(FP8X4), scales=hs_s[g][:, c0:c1], in_=hb[:, PACK * c0 : PACK * c1])
 
-        for e in range(E):
-            w1q = [load_w1(e, o, e == E - 1 and o == PASSES - 1) for o in range(PASSES)]
-            hq = layer1_routed(e, w1q)
-            w2q = load_w2(e)
-            layer2_routed(e, w2q, hq)
-            if e in [1, 2]:
-                layer1_shared([1, 2].index(e))
-
         spans = ((0, 512), (512, T))
-        banks = [[psum.tile([P, c1 - c0], F32, name="bank_s") for c0, c1 in spans] for h in range(2)]
+        banks = {}
 
-        def shared_pass(g, h, cw, cs):
+        def shared_pass(g, h, cw, cs, first):
             for i, (c0, c1) in enumerate(spans):
+                if first:
+                    banks[h, i] = psum.tile([P, c1 - c0], F32, name="bank_s")
                 nc.tensor.matmul_mx(
-                    out=banks[h][i][:],
+                    out=banks[h, i][:],
                     lhsT=cw.bitcast(FP8X4),
                     lhsT_scale=cs,
                     rhs=hs_w[g][:, c0:c1].bitcast(FP8X4),
                     rhs_scale=hs_s[g][:, c0:c1],
-                    start=(g == 0),
-                    stop=(g == PASSES - 1),
+                    start=first,
+                    stop=not first,
                 )
 
-        for g in range(PASSES):
+        def layer2_shared(g, engines):
             raw = raws.tile([P, PACK, N], F32, name="raw")
             nc.sync.dma_start(out=raw[:], in_=w2[SHARED, g * KP : (g + 1) * KP, :].rearrange("(p j) n -> p j n", j=PACK))
-            if g == 0:
-                cw, cs = quantise(cast_w2(raw[:], "s", N)[:], N, "w2q", codes)
+            if len(engines) == 1:
+                cw, cs = quantise(cast_w2(raw[:], engines, N)[:], N, "w2q", codes)
                 for h in range(2):
-                    shared_pass(g, h, cw[:, h * P : (h + 1) * P], cs[:, h * P : (h + 1) * P])
+                    shared_pass(g, h, cw[:, h * P : (h + 1) * P], cs[:, h * P : (h + 1) * P], g == 0)
             else:
-                bs = [cast_w2(raw[:, :, h * P : (h + 1) * P], "vs"[h], P) for h in range(2)]
+                bs = [cast_w2(raw[:, :, h * P : (h + 1) * P], engines[h], P) for h in range(2)]
                 for h in range(2):
                     cw, cs = quantise(bs[h][:], P, "w2q", codes)
-                    shared_pass(g, h, cw[:], cs[:])
+                    shared_pass(g, h, cw[:], cs[:], g == 0)
+
+        w1q = {}
+        hq = {}
+        w2q = {}
+        for step in ORDER:
+            kind, e = step[0], int(step[1])
+            if kind == "a" or kind == "A":
+                w1q.setdefault(e, []).append(load_w1(e, int(step[2]), step[3:], kind == "A"))
+            elif kind == "h":
+                hq[e] = layer1_routed(e, w1q[e])
+            elif kind == "s":
+                layer1_shared(e, w1q[SHARED])
+            elif kind == "b":
+                w2q[e] = load_w2(e, step[2:])
+            elif kind == "y":
+                layer2_routed(e, w2q[e], hq[e])
+            elif kind == "c":
+                layer2_shared(e, step[2:])
+            else:
+                nc.sync.dma_start(out=gate_sb[:], in_=gate[0:P, :])
         for h in range(2):
             res = keep.tile([P, T], F32, name="res%d" % h)
             for i, (c0, c1) in enumerate(spans):
-                nc.vector.tensor_tensor(res[:, c0:c1], banks[h][i][:], routed[h][:, c0:c1], ADD)
+                nc.vector.tensor_tensor(res[:, c0:c1], banks[h, i][:], routed[h][:, c0:c1], ADD)
             nc.sync.dma_start(out=out[h * P : (h + 1) * P, :], in_=res[:])

@@ -22,16 +22,16 @@ PACK = 4
 KP = P * PACK
 PASSES = 2
 SHARED = E
-ORDER = ["a40sssv","a41sssv","g0","a00sssv","a01svvv","h0","b0sv","y0","a10sssv","a11svvv","h1","b1sv","y1","s0","s1","a20sssv","a21svvv","h2","a30svvv","A31svsv","h3","b2sv","y2","b3sv","y3","c0s","c1ss"]
+ORDER = ["a40svsv","a41svsv","g0","a00vvvv","s0","s1","a01svvv","b0sv","h0","a10svsv","y0","a11svsv","b1sv","h1","a20svsv","y1","a21svsv","a30svsv","h2","b2sv","y2","A31svsv","b3sv","h3","c0v","c1ss","y3"]
 
 
 def tile_moe_shr_mlp_gelu_kernel(tc, x_words, x_scales, w1, w2, gate, offs, out):
     nc = tc.nc
     with ExitStack() as ctx:
         keep = ctx.enter_context(tc.tile_pool(name="keep", bufs=1))
-        raws = ctx.enter_context(tc.tile_pool(name="raws", bufs=8))
+        raws = ctx.enter_context(tc.tile_pool(name="raws", bufs=7))
         stage = ctx.enter_context(tc.tile_pool(name="stage", bufs=4))
-        codes = ctx.enter_context(tc.tile_pool(name="codes", bufs=6))
+        codes = ctx.enter_context(tc.tile_pool(name="codes", bufs=7))
         two = ctx.enter_context(tc.tile_pool(name="two", bufs=2))
         psum = ctx.enter_context(tc.psum_pool(name="psum", bufs=4))
 
@@ -75,8 +75,11 @@ def tile_moe_shr_mlp_gelu_kernel(tc, x_words, x_scales, w1, w2, gate, offs, out)
             nc.vector.quantize_mx(out=cw[:].bitcast(FP8X4), scales=cs[:], in_=src)
             return cw, cs
 
-        def cast_w1(raw, engines):
-            b = stage.tile([P, PACK * KP], BF16, name="w1b", align_bytes=64)
+        def cast_w1(raw, engines, held):
+            if held:
+                b = stage.tile([P, PACK * KP], BF16, name="held_h", align_bytes=64, bufs=1)
+            else:
+                b = stage.tile([P, PACK * KP], BF16, name="w1b", align_bytes=64)
             dst = b[:].rearrange("p (u t m j) -> p u m j t", u=2, t=2, j=PACK)
             src = raw.rearrange("p j (m u t) -> p u m j t", u=2, t=2)
             for u in range(2):
@@ -90,25 +93,36 @@ def tile_moe_shr_mlp_gelu_kernel(tc, x_words, x_scales, w1, w2, gate, offs, out)
             if not split:
                 raw = raws.tile([P, PACK, H], F32, name="raw")
                 nc.sync.dma_start(out=raw[:], in_=rows)
-                b = {g: cast_w1(raw[:, :, g * KP : (g + 1) * KP], engines[2 * g : 2 * g + 2]) for g in (1, 0)}
+                b = {g: cast_w1(raw[:, :, g * KP : (g + 1) * KP], engines[2 * g : 2 * g + 2], (e, o, g) == (E - 1, 0, 1)) for g in (1, 0)}
                 for g in (1, 0):
                     q[g] = quantise(b[g][:], KP, tag, pool)
             else:
                 for g in (1, 0):
                     raw = raws.tile([P, PACK, KP], F32, name="raw")
                     nc.sync.dma_start(out=raw[:], in_=rows[:, :, g * KP : (g + 1) * KP])
-                    q[g] = quantise(cast_w1(raw[:], engines[2 * g : 2 * g + 2])[:], KP, tag, pool)
+                    cw = pool.tile([P, KP], U32, name=tag + "_w", align_bytes=64)
+                    cs = pool.tile([P, KP], U8, name=tag + "_s", align_bytes=64)
+                    src = raw[:].rearrange("p j (m u t) -> p u m j t", u=2, t=2)
+                    bs = []
+                    for u in range(2):
+                        b = stage.tile([P, 2 * KP], BF16, name="w2b", align_bytes=64, bufs=7)
+                        copy_on(engines[2 * g + u], b[:].rearrange("p (t m j) -> p m j t", t=2, j=PACK), src[:, u])
+                        bs.append(b)
+                    for u in range(2):
+                        cols = slice(u * 2 * P, (u + 1) * 2 * P)
+                        nc.vector.quantize_mx(out=cw[:, cols].bitcast(FP8X4), scales=cs[:, cols], in_=bs[u][:])
+                    q[g] = (cw, cs)
             return q
 
-        def cast_w2(raw, engine, width):
-            b = stage.tile([P, PACK * width], BF16, name="w2b", align_bytes=64)
+        def cast_w2(raw, engine, width, tag="w2b", bufs=7):
+            b = stage.tile([P, PACK * width], BF16, name=tag, align_bytes=64, bufs=bufs)
             copy_on(engine, b[:].rearrange("p (c i j) -> p c j i", i=2, j=PACK), raw.rearrange("p j (c i) -> p c j i", i=2))
             return b
 
         def load_w2(e, engines):
             raw = raws.tile([P, PASSES, PACK, N], F32, name="raw")
             nc.sync.dma_start(out=raw[:].rearrange("p o j n -> p o (j n)"), in_=w2[e].rearrange("(o p j) n -> p o (j n)", o=PASSES, j=PACK))
-            b = {o: cast_w2(raw[:, o], engines[o], N) for o in (1, 0)}
+            b = {o: cast_w2(raw[:, o], engines[o], N, *(("held_h", 1) if e != 2 and o == 0 else ())) for o in (1, 0)}
             return {o: quantise(b[o][:], N, "w2q", codes) for o in (1, 0)}
 
         def layer1_block(w1q, g, words, scales, width, c0, hb, tag):
@@ -130,7 +144,10 @@ def tile_moe_shr_mlp_gelu_kernel(tc, x_words, x_scales, w1, w2, gate, offs, out)
         def layer1_routed(e, w1q):
             hq = {}
             for g in (1, 0):
-                hb = stage.tile([P, PACK * C], BF16, name="hb", align_bytes=64)
+                if g == 0:
+                    hb = stage.tile([P, PACK * C], BF16, name="held_h", align_bytes=64, bufs=1)
+                else:
+                    hb = stage.tile([P, PACK * C], BF16, name="hb", align_bytes=64)
                 layer1_block(w1q, g, gw, gs, S, e * C, hb[:], "bank")
                 hq[g] = quantise(hb[:], C, "hq", codes)
             return hq
@@ -143,13 +160,16 @@ def tile_moe_shr_mlp_gelu_kernel(tc, x_words, x_scales, w1, w2, gate, offs, out)
                         out=bank[:, h, :],
                         lhsT=w2q[g][0][:, h * P : (h + 1) * P].bitcast(FP8X4),
                         lhsT_scale=w2q[g][1][:, h * P : (h + 1) * P],
-                        rhs=hq[g][0][:].bitcast(FP8X4),
-                        rhs_scale=hq[g][1][:],
+                        rhs=hq[g][0][:, 0:C].bitcast(FP8X4),
+                        rhs_scale=hq[g][1][:, 0:C],
                         start=(g == 1),
                         stop=(g == 0),
                     )
-            y = stage.tile([P, 2, C], F32, name="y")
-            copy_on("s", y[:], bank[:])
+            if e == E - 1:
+                y = stage.tile([P, 2, C], F32, name="held_y", align_bytes=64, bufs=1)
+            else:
+                y = stage.tile([P, 2, C], F32, name="y")
+            copy_on("sssv"[e], y[:], bank[:])
             lst = offsets[:, e * C // 16 : (e + 1) * C // 16]
             for h in range(2):
                 nc.vector.tensor_tensor(routed[h][:].indirect(lst), y[:, h, :], gate_sb[:, e * C : (e + 1) * C], MULT)
@@ -189,7 +209,7 @@ def tile_moe_shr_mlp_gelu_kernel(tc, x_words, x_scales, w1, w2, gate, offs, out)
                 for h in range(2):
                     shared_pass(g, h, cw[:, h * P : (h + 1) * P], cs[:, h * P : (h + 1) * P], g == 0)
             else:
-                bs = [cast_w2(raw[:, :, h * P : (h + 1) * P], engines[h], P) for h in range(2)]
+                bs = [cast_w2(raw[:, :, h * P : (h + 1) * P], engines[h], P, *(("held_y", 1) if h == 1 else ())) for h in range(2)]
                 for h in range(2):
                     cw, cs = quantise(bs[h][:], P, "w2q", codes)
                     shared_pass(g, h, cw[:], cs[:], g == 0)
@@ -217,4 +237,4 @@ def tile_moe_shr_mlp_gelu_kernel(tc, x_words, x_scales, w1, w2, gate, offs, out)
             res = keep.tile([P, T], F32, name="res%d" % h)
             for i, (c0, c1) in enumerate(spans):
                 nc.vector.tensor_tensor(res[:, c0:c1], banks[h, i][:], routed[h][:, c0:c1], ADD)
-            nc.sync.dma_start(out=out[h * P : (h + 1) * P, :], in_=res[:])
+                nc.sync.dma_start(out=out[h * P : (h + 1) * P, c0:c1], in_=res[:, c0:c1])

@@ -1,10 +1,13 @@
 from contextlib import ExitStack
 
 import concourse.mybir as mybir
+from concourse.masks import make_identity
 
 K, T, E, C, H, N = 1024, 640, 4, 128, 1024, 256
-S = E * C
-FLOPS = 2 * (S + T) * (K * H + H * N)
+SLOTS = E * C
+SHARED = E
+LAST = E - 1
+FLOPS = 2 * (SLOTS + T) * (K * H + H * N)
 
 F32 = mybir.dt.float32
 BF16 = mybir.dt.bfloat16
@@ -21,12 +24,19 @@ P = 128
 PACK = 4
 KP = P * PACK
 PASSES = 2
-SHARED = E
-ORDER = ["a40svsv","a41svsv","g0","a00vvvv","s0","s1","a01svvv","b0sv","h0","a10svsv","y0","a11svsv","b1sv","h1","a20svsv","y1","a21svsv","a30svsv","h2","b2sv","y2","A31svsv","b3sv","h3","c0v","c1ss","y3"]
+HALVES = N // P
+PER_COLUMN = 16
+SPANS = ((0, 512), (512, T))
+BACKWARDS = (1, 0)
 
 
 def tile_moe_shr_mlp_gelu_kernel(tc, x_words, x_scales, w1, w2, gate, offs, out):
     nc = tc.nc
+    on_scalar, on_vector = nc.scalar.copy, nc.vector.tensor_copy
+    even = (on_scalar, on_vector, on_scalar, on_vector)
+    all_vector = (on_vector,) * 4
+    mostly_vector = (on_scalar, on_vector, on_vector, on_vector)
+
     with ExitStack() as ctx:
         keep = ctx.enter_context(tc.tile_pool(name="keep", bufs=1))
         raws = ctx.enter_context(tc.tile_pool(name="raws", bufs=7))
@@ -35,13 +45,13 @@ def tile_moe_shr_mlp_gelu_kernel(tc, x_words, x_scales, w1, w2, gate, offs, out)
         two = ctx.enter_context(tc.tile_pool(name="two", bufs=2))
         psum = ctx.enter_context(tc.psum_pool(name="psum", bufs=4))
 
-        offsets = keep.tile([P, S // 16], U16, name="offsets")
+        offsets = keep.tile([P, SLOTS // PER_COLUMN], U16, name="offsets")
         xw = keep.tile([P, PASSES * T], U32, name="xw", align_bytes=64)
         xs = keep.tile([P, T], U8, name="xs", align_bytes=64)
-        gw = keep.tile([P, PASSES * S], U32, name="gw", align_bytes=64)
-        gs = keep.tile([P, S], U8, name="gs", align_bytes=64)
-        gate_sb = keep.tile([P, S], F32, name="gate_sb")
-        routed = [keep.tile([P, T], F32, name="routed%d" % h) for h in range(2)]
+        gw = keep.tile([P, PASSES * SLOTS], U32, name="gw", align_bytes=64)
+        gs = keep.tile([P, SLOTS], U8, name="gs", align_bytes=64)
+        gate_sb = keep.tile([P, SLOTS], F32, name="gate_sb")
+        routed = [keep.tile([P, T], F32, name="routed%d" % h) for h in range(HALVES)]
 
         nc.vector.memset(xs[:].bitcast(I32), 0)
         nc.sync.dma_start(
@@ -51,190 +61,218 @@ def tile_moe_shr_mlp_gelu_kernel(tc, x_words, x_scales, w1, w2, gate, offs, out)
         nc.sync.dma_start(offsets[:], offs)
         for q in range(4):
             nc.sync.dma_start(
-                out=xs[32 * q : 32 * q + 8, :].bitcast(I32),
+                out=xs[32 * q : 32 * q + 4 * PASSES, :].bitcast(I32),
                 in_=x_scales[:, 4 * q : 4 * q + 4, :].bitcast(I32),
             )
-        for h in range(2):
+        for h in range(HALVES):
             nc.vector.memset(routed[h][:], 0.0)
-        half = S // 2
-        for a in range(2):
-            lst = offsets[:, a * half // 16 : (a + 1) * half // 16]
+        pair = 2 * C
+        for s0 in range(0, SLOTS, pair):
+            entries = offsets[:, s0 // PER_COLUMN : (s0 + pair) // PER_COLUMN]
             for o in range(PASSES):
-                nc.vector.tensor_copy(gw[:, o * S + a * half : o * S + (a + 1) * half], xw[:, o * T : (o + 1) * T].indirect(lst))
-            nc.vector.tensor_copy(gs[:, a * half : (a + 1) * half], xs[:].indirect(lst))
+                nc.vector.tensor_copy(
+                    gw[:, o * SLOTS + s0 : o * SLOTS + s0 + pair], xw[:, o * T : (o + 1) * T].indirect(entries)
+                )
+            nc.vector.tensor_copy(gs[:, s0 : s0 + pair], xs[:].indirect(entries))
 
-        def copy_on(engine, dst, src):
-            if engine == "s":
-                nc.scalar.copy(dst, src)
-            else:
-                nc.vector.tensor_copy(dst, src)
+        def staged(shape, dtype, tag):
+            bufs = {"held_h": 1, "held_y": 1, "small": 7}.get(tag, 4)
+            return stage.tile(shape, dtype, name=tag, align_bytes=64, bufs=bufs)
 
-        def quantise(src, width, tag, pool):
-            cw = pool.tile([P, width], U32, name=tag + "_w", align_bytes=64)
-            cs = pool.tile([P, width], U8, name=tag + "_s", align_bytes=64)
-            nc.vector.quantize_mx(out=cw[:].bitcast(FP8X4), scales=cs[:], in_=src)
-            return cw, cs
+        def code_tiles(width, tag, pool):
+            words = pool.tile([P, width], U32, name=tag + "_w", align_bytes=64)
+            scales = pool.tile([P, width], U8, name=tag + "_s", align_bytes=64)
+            return words, scales
 
-        def cast_w1(raw, engines, held):
-            if held:
-                b = stage.tile([P, PACK * KP], BF16, name="held_h", align_bytes=64, bufs=1)
-            else:
-                b = stage.tile([P, PACK * KP], BF16, name="w1b", align_bytes=64)
-            dst = b[:].rearrange("p (u t m j) -> p u m j t", u=2, t=2, j=PACK)
-            src = raw.rearrange("p j (m u t) -> p u m j t", u=2, t=2)
-            for u in range(2):
-                copy_on(engines[u], dst[:, u], src[:, u])
-            return b
+        def quantise(rounded, width, tag, pool):
+            words, scales = code_tiles(width, tag, pool)
+            nc.vector.quantize_mx(out=words[:].bitcast(FP8X4), scales=scales[:], in_=rounded[:])
+            return words, scales
 
-        def load_w1(e, o, engines, split):
+        def w1_rows(e, o):
+            return w1[e, o * KP : (o + 1) * KP, :].rearrange("(p j) c -> p j c", j=PACK)
+
+        def by_quarter(raw):
+            return raw.rearrange("p j (m u t) -> p u m j t", u=2, t=2)
+
+        def load_w1(e, o, copies, hold=False):
             tag, pool = ("w1s%d" % o, two) if e == SHARED else ("w1q", codes)
-            rows = w1[e, o * KP : (o + 1) * KP, :].rearrange("(p j) c -> p j c", j=PACK)
-            q = {}
-            if not split:
-                raw = raws.tile([P, PACK, H], F32, name="raw")
-                nc.sync.dma_start(out=raw[:], in_=rows)
-                b = {g: cast_w1(raw[:, :, g * KP : (g + 1) * KP], engines[2 * g : 2 * g + 2], (e, o, g) == (E - 1, 0, 1)) for g in (1, 0)}
-                for g in (1, 0):
-                    q[g] = quantise(b[g][:], KP, tag, pool)
-            else:
-                for g in (1, 0):
-                    raw = raws.tile([P, PACK, KP], F32, name="raw")
-                    nc.sync.dma_start(out=raw[:], in_=rows[:, :, g * KP : (g + 1) * KP])
-                    cw = pool.tile([P, KP], U32, name=tag + "_w", align_bytes=64)
-                    cs = pool.tile([P, KP], U8, name=tag + "_s", align_bytes=64)
-                    src = raw[:].rearrange("p j (m u t) -> p u m j t", u=2, t=2)
-                    bs = []
-                    for u in range(2):
-                        b = stage.tile([P, 2 * KP], BF16, name="w2b", align_bytes=64, bufs=7)
-                        copy_on(engines[2 * g + u], b[:].rearrange("p (t m j) -> p m j t", t=2, j=PACK), src[:, u])
-                        bs.append(b)
-                    for u in range(2):
-                        cols = slice(u * 2 * P, (u + 1) * 2 * P)
-                        nc.vector.quantize_mx(out=cw[:, cols].bitcast(FP8X4), scales=cs[:, cols], in_=bs[u][:])
-                    q[g] = (cw, cs)
-            return q
+            raw = raws.tile([P, PACK, H], F32, name="raw")
+            nc.sync.dma_start(out=raw[:], in_=w1_rows(e, o))
+            rounded = {}
+            for g in BACKWARDS:
+                rounded[g] = staged([P, PACK * KP], BF16, "held_h" if hold and g == 1 else "w1b")
+                dst = rounded[g][:].rearrange("p (u t m j) -> p u m j t", u=2, t=2, j=PACK)
+                src = by_quarter(raw[:, :, g * KP : (g + 1) * KP])
+                for u in range(2):
+                    copies[2 * g + u](dst[:, u], src[:, u])
+            return {g: quantise(rounded[g], KP, tag, pool) for g in BACKWARDS}
 
-        def cast_w2(raw, engine, width, tag="w2b", bufs=7):
-            b = stage.tile([P, PACK * width], BF16, name=tag, align_bytes=64, bufs=bufs)
-            copy_on(engine, b[:].rearrange("p (c i j) -> p c j i", i=2, j=PACK), raw.rearrange("p j (c i) -> p c j i", i=2))
-            return b
+        def load_last_w1():
+            quantised = {}
+            for g in BACKWARDS:
+                raw = raws.tile([P, PACK, KP], F32, name="raw")
+                nc.sync.dma_start(out=raw[:], in_=w1_rows(LAST, 1)[:, :, g * KP : (g + 1) * KP])
+                words, scales = code_tiles(KP, "w1q", codes)
+                src = by_quarter(raw[:])
+                quarters = []
+                for u in range(2):
+                    rounded = staged([P, 2 * KP], BF16, "small")
+                    even[2 * g + u](rounded[:].rearrange("p (t m j) -> p m j t", t=2, j=PACK), src[:, u])
+                    quarters.append(rounded)
+                for u in range(2):
+                    cols = slice(u * 2 * P, (u + 1) * 2 * P)
+                    nc.vector.quantize_mx(out=words[:, cols].bitcast(FP8X4), scales=scales[:, cols], in_=quarters[u][:])
+                quantised[g] = (words, scales)
+            return quantised
 
-        def load_w2(e, engines):
+        def round_w2(raw, copy, width, tag):
+            rounded = staged([P, PACK * width], BF16, tag)
+            copy(rounded[:].rearrange("p (c i j) -> p c j i", i=2, j=PACK), raw.rearrange("p j (c i) -> p c j i", i=2))
+            return rounded
+
+        def load_w2(e, hold):
             raw = raws.tile([P, PASSES, PACK, N], F32, name="raw")
-            nc.sync.dma_start(out=raw[:].rearrange("p o j n -> p o (j n)"), in_=w2[e].rearrange("(o p j) n -> p o (j n)", o=PASSES, j=PACK))
-            b = {o: cast_w2(raw[:, o], engines[o], N, *(("held_h", 1) if e != 2 and o == 0 else ())) for o in (1, 0)}
-            return {o: quantise(b[o][:], N, "w2q", codes) for o in (1, 0)}
+            nc.sync.dma_start(
+                out=raw[:].rearrange("p o j n -> p o (j n)"),
+                in_=w2[e].rearrange("(o p j) n -> p o (j n)", o=PASSES, j=PACK),
+            )
+            rounded = {
+                1: round_w2(raw[:, 1], on_vector, N, "small"),
+                0: round_w2(raw[:, 0], on_scalar, N, "held_h" if hold else "small"),
+            }
+            return {o: quantise(rounded[o], N, "w2q", codes) for o in BACKWARDS}
 
-        def layer1_block(w1q, g, words, scales, width, c0, hb, tag):
+        def hidden_block(w1q, g, words, scales, width, c0, hidden, tag):
             bank = psum.tile([P, PACK, C], F32, name=tag)
             for t in range(PACK):
                 for o in range(PASSES):
-                    cw, cs = w1q[o][g]
+                    w_words, w_scales = w1q[o][g]
                     nc.tensor.matmul_mx(
                         out=bank[:, t, :],
-                        lhsT=cw[:, t * P : (t + 1) * P].bitcast(FP8X4),
-                        lhsT_scale=cs[:, t * P : (t + 1) * P],
+                        lhsT=w_words[:, t * P : (t + 1) * P].bitcast(FP8X4),
+                        lhsT_scale=w_scales[:, t * P : (t + 1) * P],
                         rhs=words[:, o * width + c0 : o * width + c0 + C].bitcast(FP8X4),
                         rhs_scale=scales[4 * o : P, c0 : c0 + C],
                         start=(o == 0),
                         stop=(o == PASSES - 1),
                     )
-            nc.scalar.activation(hb.rearrange("p (n t) -> p n t", t=PACK), bank[:].rearrange("p t n -> p n t"), GELU)
+            nc.scalar.activation(hidden.rearrange("p (n t) -> p n t", t=PACK), bank[:].rearrange("p t n -> p n t"), GELU)
 
-        def layer1_routed(e, w1q):
+        def first_layer(e, w1q):
             hq = {}
-            for g in (1, 0):
-                if g == 0:
-                    hb = stage.tile([P, PACK * C], BF16, name="held_h", align_bytes=64, bufs=1)
-                else:
-                    hb = stage.tile([P, PACK * C], BF16, name="hb", align_bytes=64)
-                layer1_block(w1q, g, gw, gs, S, e * C, hb[:], "bank")
-                hq[g] = quantise(hb[:], C, "hq", codes)
+            for g in BACKWARDS:
+                hidden = staged([P, PACK * C], BF16, "held_h" if g == 0 else "hb")
+                hidden_block(w1q, g, gw, gs, SLOTS, e * C, hidden[:], "bank")
+                hq[g] = quantise(hidden, C, "hq", codes)
             return hq
 
-        def layer2_routed(e, w2q, hq):
-            bank = psum.tile([P, 2, C], F32, name="bank")
-            for h in range(2):
-                for g in (1, 0):
+        def second_layer(e, w2q, hq):
+            bank = psum.tile([P, HALVES, C], F32, name="bank")
+            for h in range(HALVES):
+                for g in BACKWARDS:
                     nc.tensor.matmul_mx(
                         out=bank[:, h, :],
                         lhsT=w2q[g][0][:, h * P : (h + 1) * P].bitcast(FP8X4),
                         lhsT_scale=w2q[g][1][:, h * P : (h + 1) * P],
-                        rhs=hq[g][0][:, 0:C].bitcast(FP8X4),
-                        rhs_scale=hq[g][1][:, 0:C],
+                        rhs=hq[g][0][:].bitcast(FP8X4),
+                        rhs_scale=hq[g][1][:],
                         start=(g == 1),
                         stop=(g == 0),
                     )
-            if e == E - 1:
-                y = stage.tile([P, 2, C], F32, name="held_y", align_bytes=64, bufs=1)
-            else:
-                y = stage.tile([P, 2, C], F32, name="y")
-            copy_on("sssv"[e], y[:], bank[:])
-            lst = offsets[:, e * C // 16 : (e + 1) * C // 16]
-            for h in range(2):
-                nc.vector.tensor_tensor(routed[h][:].indirect(lst), y[:, h, :], gate_sb[:, e * C : (e + 1) * C], MULT)
+            y = staged([P, HALVES, C], F32, "held_y" if e == LAST else "y")
+            (on_vector if e == LAST else on_scalar)(y[:], bank[:])
+            entries = offsets[:, e * C // PER_COLUMN : (e + 1) * C // PER_COLUMN]
+            for h in range(HALVES):
+                nc.vector.tensor_tensor(routed[h][:].indirect(entries), y[:, h, :], gate_sb[:, e * C : (e + 1) * C], MULT)
 
         hs_w = [keep.tile([P, T], U32, name="hs_w%d" % g, align_bytes=64) for g in range(PASSES)]
         hs_s = [keep.tile([P, T], U8, name="hs_s%d" % g, align_bytes=64) for g in range(PASSES)]
 
-        def layer1_shared(g, w1q):
-            hb = keep.tile([P, PACK * T], BF16, name="hsb%d" % g, align_bytes=64)
-            for b in range(T // C):
-                layer1_block(w1q, g, xw, xs, T, b * C, hb[:, b * PACK * C : (b + 1) * PACK * C], "bank_s")
-            for c0, c1 in ((0, 512), (512, T)):
-                nc.vector.quantize_mx(out=hs_w[g][:, c0:c1].bitcast(FP8X4), scales=hs_s[g][:, c0:c1], in_=hb[:, PACK * c0 : PACK * c1])
-
-        spans = ((0, 512), (512, T))
-        banks = {}
-
-        def shared_pass(g, h, cw, cs, first):
-            for i, (c0, c1) in enumerate(spans):
-                if first:
-                    banks[h, i] = psum.tile([P, c1 - c0], F32, name="bank_s")
-                nc.tensor.matmul_mx(
-                    out=banks[h, i][:],
-                    lhsT=cw.bitcast(FP8X4),
-                    lhsT_scale=cs,
-                    rhs=hs_w[g][:, c0:c1].bitcast(FP8X4),
-                    rhs_scale=hs_s[g][:, c0:c1],
-                    start=first,
-                    stop=not first,
+        def shared_first_layer(g, w1q):
+            hidden = keep.tile([P, PACK * T], BF16, name="hsb%d" % g, align_bytes=64)
+            for c0 in range(0, T, C):
+                hidden_block(w1q, g, xw, xs, T, c0, hidden[:, PACK * c0 : PACK * (c0 + C)], "bank_s")
+            for c0, c1 in SPANS:
+                nc.vector.quantize_mx(
+                    out=hs_w[g][:, c0:c1].bitcast(FP8X4), scales=hs_s[g][:, c0:c1], in_=hidden[:, PACK * c0 : PACK * c1]
                 )
 
-        def layer2_shared(g, engines):
+        ys = {}
+
+        def shared_pass(g, h, w_words, w_scales):
+            for c0, c1 in SPANS:
+                if g == 0:
+                    ys[h, c0] = psum.tile([P, c1 - c0], F32, name="bank_s")
+                nc.tensor.matmul_mx(
+                    out=ys[h, c0][:],
+                    lhsT=w_words.bitcast(FP8X4),
+                    lhsT_scale=w_scales,
+                    rhs=hs_w[g][:, c0:c1].bitcast(FP8X4),
+                    rhs_scale=hs_s[g][:, c0:c1],
+                    start=(g == 0),
+                    stop=(g == PASSES - 1),
+                )
+
+        def load_shared_w2(g):
             raw = raws.tile([P, PACK, N], F32, name="raw")
             nc.sync.dma_start(out=raw[:], in_=w2[SHARED, g * KP : (g + 1) * KP, :].rearrange("(p j) n -> p j n", j=PACK))
-            if len(engines) == 1:
-                cw, cs = quantise(cast_w2(raw[:], engines, N)[:], N, "w2q", codes)
-                for h in range(2):
-                    shared_pass(g, h, cw[:, h * P : (h + 1) * P], cs[:, h * P : (h + 1) * P], g == 0)
-            else:
-                bs = [cast_w2(raw[:, :, h * P : (h + 1) * P], engines[h], P, *(("held_y", 1) if h == 1 else ())) for h in range(2)]
-                for h in range(2):
-                    cw, cs = quantise(bs[h][:], P, "w2q", codes)
-                    shared_pass(g, h, cw[:], cs[:], g == 0)
+            return raw
 
-        w1q = {}
-        hq = {}
-        w2q = {}
-        for step in ORDER:
-            kind, e = step[0], int(step[1])
-            if kind == "a" or kind == "A":
-                w1q.setdefault(e, []).append(load_w1(e, int(step[2]), step[3:], kind == "A"))
-            elif kind == "h":
-                hq[e] = layer1_routed(e, w1q[e])
-            elif kind == "s":
-                layer1_shared(e, w1q[SHARED])
-            elif kind == "b":
-                w2q[e] = load_w2(e, step[2:])
-            elif kind == "y":
-                layer2_routed(e, w2q[e], hq[e])
-            elif kind == "c":
-                layer2_shared(e, step[2:])
+        def shared_second_layer():
+            words, scales = quantise(round_w2(load_shared_w2(0)[:], on_vector, N, "small"), N, "w2q", codes)
+            for h in range(HALVES):
+                shared_pass(0, h, words[:, h * P : (h + 1) * P], scales[:, h * P : (h + 1) * P])
+            raw = load_shared_w2(1)
+            rounded = [
+                round_w2(raw[:, :, h * P : (h + 1) * P], on_scalar, P, "held_y" if h == 1 else "small")
+                for h in range(HALVES)
+            ]
+            for h in range(HALVES):
+                words, scales = quantise(rounded[h], P, "w2q", codes)
+                shared_pass(1, h, words[:], scales[:])
+
+        def spread_gate():
+            identity = keep.tile([P, P], F32, name="identity")
+            make_identity(nc, identity[:])
+            rows = keep.tile([P, C], F32, name="gate_rows")
+            nc.vector.memset(rows[:], 0.0)
+            nc.sync.dma_start(out=rows[0:E, :], in_=gate[0, :].rearrange("(e c) -> e c", e=E))
+            turned = psum.tile([P, P], F32, name="bank")
+            nc.tensor.transpose(turned[:], rows[:], identity[:])
+            columns = keep.tile([P, E], F32, name="gate_columns")
+            nc.scalar.copy(columns[:], turned[:, 0:E])
+            spread = psum.tile([P, E, C], F32, name="bank")
+            for e in range(E):
+                nc.tensor.transpose(spread[:, e, :], columns[:, e : e + 1].to_broadcast([P, P]), identity[:])
+            nc.scalar.copy(gate_sb[:].rearrange("p (e c) -> p e c", e=E), spread[:])
+
+        spread_gate()
+        shared_w1q = [load_w1(SHARED, o, even) for o in range(PASSES)]
+        first_pass = load_w1(0, 0, all_vector)
+        for g in range(PASSES):
+            shared_first_layer(g, shared_w1q)
+
+        for e in range(E):
+            if e == LAST:
+                w1q = [first_pass, load_last_w1()]
             else:
-                nc.sync.dma_start(out=gate_sb[:], in_=gate[0:P, :])
-        for h in range(2):
-            res = keep.tile([P, T], F32, name="res%d" % h)
-            for i, (c0, c1) in enumerate(spans):
-                nc.vector.tensor_tensor(res[:, c0:c1], banks[h, i][:], routed[h][:, c0:c1], ADD)
-                nc.sync.dma_start(out=out[h * P : (h + 1) * P, c0:c1], in_=res[:, c0:c1])
+                w1q = [first_pass, load_w1(e, 1, mostly_vector if e == 0 else even)]
+            if e == LAST - 1:
+                first_pass = load_w1(LAST, 0, even, hold=True)
+                hq = first_layer(e, w1q)
+                w2q = load_w2(e, hold=False)
+            else:
+                w2q = load_w2(e, hold=True)
+                hq = first_layer(e, w1q)
+                if e == LAST:
+                    shared_second_layer()
+                else:
+                    first_pass = load_w1(e + 1, 0, even)
+            second_layer(e, w2q, hq)
+
+        for h in range(HALVES):
+            result = keep.tile([P, T], F32, name="result%d" % h)
+            for c0, c1 in SPANS:
+                nc.vector.tensor_tensor(result[:, c0:c1], ys[h, c0][:], routed[h][:, c0:c1], ADD)
+                nc.sync.dma_start(out=out[h * P : (h + 1) * P, c0:c1], in_=result[:, c0:c1])

@@ -51,12 +51,12 @@ def tile_moe_shr_mlp_gelu_kernel(tc, x_words, x_scales, w1, w2, gate, offs, out)
         gw = keep.tile([P, PASSES * SLOTS], U32, name="gw", align_bytes=64)
         gs = keep.tile([P, SLOTS], U8, name="gs", align_bytes=64)
         gate_sb = keep.tile([P, SLOTS], F32, name="gate_sb")
-        routed = [keep.tile([P, T], F32, name="routed%d" % h) for h in range(HALVES)]
+        routed = [keep.tile([P, T], F32, name="routed%d" % r) for r in range(HALVES)]
 
         nc.vector.memset(xs[:].bitcast(I32), 0)
         nc.sync.dma_start(
-            out=xw[:].bitcast(I32).rearrange("p (o t) -> p o t", o=PASSES),
-            in_=x_words.rearrange("o p t r -> p o (t r)").bitcast(I32),
+            out=xw[:].bitcast(I32).rearrange("p (o c) -> p o c", o=PASSES),
+            in_=x_words.rearrange("o p c j -> p o (c j)").bitcast(I32),
         )
         nc.sync.dma_start(offsets[:], offs)
         for q in range(4):
@@ -64,8 +64,10 @@ def tile_moe_shr_mlp_gelu_kernel(tc, x_words, x_scales, w1, w2, gate, offs, out)
                 out=xs[32 * q : 32 * q + 4 * PASSES, :].bitcast(I32),
                 in_=x_scales[:, 4 * q : 4 * q + 4, :].bitcast(I32),
             )
-        for h in range(HALVES):
-            nc.vector.memset(routed[h][:], 0.0)
+        for r in range(HALVES):
+            nc.vector.memset(routed[r][:], 0.0)
+        warm = keep.tile([P, 1], F32, name="warm")
+        nc.scalar.activation(warm[:], routed[0][:, 0:1], GELU)
         pair = 2 * C
         for s0 in range(0, SLOTS, pair):
             entries = offsets[:, s0 // PER_COLUMN : (s0 + pair) // PER_COLUMN]
@@ -76,7 +78,7 @@ def tile_moe_shr_mlp_gelu_kernel(tc, x_words, x_scales, w1, w2, gate, offs, out)
             nc.vector.tensor_copy(gs[:, s0 : s0 + pair], xs[:].indirect(entries))
 
         def staged(shape, dtype, tag):
-            bufs = {"held_h": 1, "held_y": 1, "small": 7}.get(tag, 4)
+            bufs = {"held_h": 1, "held_y": 1, "y": 1, "small": 7}.get(tag, 4)
             return stage.tile(shape, dtype, name=tag, align_bytes=64, bufs=bufs)
 
         def code_tiles(width, tag, pool):
@@ -93,16 +95,16 @@ def tile_moe_shr_mlp_gelu_kernel(tc, x_words, x_scales, w1, w2, gate, offs, out)
             return w1[e, o * KP : (o + 1) * KP, :].rearrange("(p j) c -> p j c", j=PACK)
 
         def by_quarter(raw):
-            return raw.rearrange("p j (m u t) -> p u m j t", u=2, t=2)
+            return raw.rearrange("p j (m u v) -> p u m j v", u=2, v=2)
 
-        def load_w1(e, o, copies, hold=False):
+        def load_w1(e, o, copies, hold=None):
             tag, pool = ("w1s%d" % o, two) if e == SHARED else ("w1q", codes)
             raw = raws.tile([P, PACK, H], F32, name="raw")
             nc.sync.dma_start(out=raw[:], in_=w1_rows(e, o))
             rounded = {}
             for g in BACKWARDS:
-                rounded[g] = staged([P, PACK * KP], BF16, "held_h" if hold and g == 1 else "w1b")
-                dst = rounded[g][:].rearrange("p (u t m j) -> p u m j t", u=2, t=2, j=PACK)
+                rounded[g] = staged([P, PACK * KP], BF16, hold if hold and g == 1 else "w1b")
+                dst = rounded[g][:].rearrange("p (u v m j) -> p u m j v", u=2, v=2, j=PACK)
                 src = by_quarter(raw[:, :, g * KP : (g + 1) * KP])
                 for u in range(2):
                     copies[2 * g + u](dst[:, u], src[:, u])
@@ -118,7 +120,7 @@ def tile_moe_shr_mlp_gelu_kernel(tc, x_words, x_scales, w1, w2, gate, offs, out)
                 quarters = []
                 for u in range(2):
                     rounded = staged([P, 2 * KP], BF16, "small")
-                    even[2 * g + u](rounded[:].rearrange("p (t m j) -> p m j t", t=2, j=PACK), src[:, u])
+                    even[2 * g + u](rounded[:].rearrange("p (v m j) -> p m j v", v=2, j=PACK), src[:, u])
                     quarters.append(rounded)
                 for u in range(2):
                     cols = slice(u * 2 * P, (u + 1) * 2 * P)
@@ -128,10 +130,10 @@ def tile_moe_shr_mlp_gelu_kernel(tc, x_words, x_scales, w1, w2, gate, offs, out)
 
         def round_w2(raw, copy, width, tag):
             rounded = staged([P, PACK * width], BF16, tag)
-            copy(rounded[:].rearrange("p (c i j) -> p c j i", i=2, j=PACK), raw.rearrange("p j (c i) -> p c j i", i=2))
+            copy(rounded[:].rearrange("p (c v j) -> p c j v", v=2, j=PACK), raw.rearrange("p j (c v) -> p c j v", v=2))
             return rounded
 
-        def load_w2(e, hold):
+        def load_w2(e, hold=None):
             raw = raws.tile([P, PASSES, PACK, N], F32, name="raw")
             nc.sync.dma_start(
                 out=raw[:].rearrange("p o j n -> p o (j n)"),
@@ -139,7 +141,7 @@ def tile_moe_shr_mlp_gelu_kernel(tc, x_words, x_scales, w1, w2, gate, offs, out)
             )
             rounded = {
                 1: round_w2(raw[:, 1], on_vector, N, "small"),
-                0: round_w2(raw[:, 0], on_scalar, N, "held_h" if hold else "small"),
+                0: round_w2(raw[:, 0], on_scalar, N, hold or "small"),
             }
             return {o: quantise(rounded[o], N, "w2q", codes) for o in BACKWARDS}
 
@@ -169,22 +171,22 @@ def tile_moe_shr_mlp_gelu_kernel(tc, x_words, x_scales, w1, w2, gate, offs, out)
 
         def second_layer(e, w2q, hq):
             bank = psum.tile([P, HALVES, C], F32, name="bank")
-            for h in range(HALVES):
+            for r in range(HALVES):
                 for g in BACKWARDS:
                     nc.tensor.matmul_mx(
-                        out=bank[:, h, :],
-                        lhsT=w2q[g][0][:, h * P : (h + 1) * P].bitcast(FP8X4),
-                        lhsT_scale=w2q[g][1][:, h * P : (h + 1) * P],
+                        out=bank[:, r, :],
+                        lhsT=w2q[g][0][:, r * P : (r + 1) * P].bitcast(FP8X4),
+                        lhsT_scale=w2q[g][1][:, r * P : (r + 1) * P],
                         rhs=hq[g][0][:].bitcast(FP8X4),
                         rhs_scale=hq[g][1][:],
                         start=(g == 1),
                         stop=(g == 0),
                     )
-            y = staged([P, HALVES, C], F32, "held_y" if e == LAST else "y")
+            y = staged([P, HALVES, C], F32, "y" if e == LAST - 1 else "held_y")
             (on_vector if e == LAST else on_scalar)(y[:], bank[:])
             entries = offsets[:, e * C // PER_COLUMN : (e + 1) * C // PER_COLUMN]
-            for h in range(HALVES):
-                nc.vector.tensor_tensor(routed[h][:].indirect(entries), y[:, h, :], gate_sb[:, e * C : (e + 1) * C], MULT)
+            for r in range(HALVES):
+                nc.vector.tensor_tensor(routed[r][:].indirect(entries), y[:, r, :], gate_sb[:, e * C : (e + 1) * C], MULT)
 
         hs_w = [keep.tile([P, T], U32, name="hs_w%d" % g, align_bytes=64) for g in range(PASSES)]
         hs_s = [keep.tile([P, T], U8, name="hs_s%d" % g, align_bytes=64) for g in range(PASSES)]
@@ -200,12 +202,12 @@ def tile_moe_shr_mlp_gelu_kernel(tc, x_words, x_scales, w1, w2, gate, offs, out)
 
         ys = {}
 
-        def shared_pass(g, h, w_words, w_scales):
+        def shared_pass(g, r, w_words, w_scales):
             for c0, c1 in SPANS:
                 if g == 0:
-                    ys[h, c0] = psum.tile([P, c1 - c0], F32, name="bank_s")
+                    ys[r, c0] = psum.tile([P, c1 - c0], F32, name="bank_s")
                 nc.tensor.matmul_mx(
-                    out=ys[h, c0][:],
+                    out=ys[r, c0][:],
                     lhsT=w_words.bitcast(FP8X4),
                     lhsT_scale=w_scales,
                     rhs=hs_w[g][:, c0:c1].bitcast(FP8X4),
@@ -221,16 +223,16 @@ def tile_moe_shr_mlp_gelu_kernel(tc, x_words, x_scales, w1, w2, gate, offs, out)
 
         def shared_second_layer():
             words, scales = quantise(round_w2(load_shared_w2(0)[:], on_vector, N, "small"), N, "w2q", codes)
-            for h in range(HALVES):
-                shared_pass(0, h, words[:, h * P : (h + 1) * P], scales[:, h * P : (h + 1) * P])
+            for r in range(HALVES):
+                shared_pass(0, r, words[:, r * P : (r + 1) * P], scales[:, r * P : (r + 1) * P])
             raw = load_shared_w2(1)
             rounded = [
-                round_w2(raw[:, :, h * P : (h + 1) * P], on_scalar, P, "held_y" if h == 1 else "small")
-                for h in range(HALVES)
+                round_w2(raw[:, :, r * P : (r + 1) * P], on_scalar, P, "held_y" if r == 1 else "small")
+                for r in range(HALVES)
             ]
-            for h in range(HALVES):
-                words, scales = quantise(rounded[h], P, "w2q", codes)
-                shared_pass(1, h, words[:], scales[:])
+            for r in range(HALVES):
+                words, scales = quantise(rounded[r], P, "w2q", codes)
+                shared_pass(1, r, words[:], scales[:])
 
         def spread_gate():
             identity = keep.tile([P, P], F32, name="identity")
@@ -259,20 +261,20 @@ def tile_moe_shr_mlp_gelu_kernel(tc, x_words, x_scales, w1, w2, gate, offs, out)
             else:
                 w1q = [first_pass, load_w1(e, 1, mostly_vector if e == 0 else even)]
             if e == LAST - 1:
-                first_pass = load_w1(LAST, 0, even, hold=True)
+                first_pass = load_w1(LAST, 0, even, hold="held_h")
                 hq = first_layer(e, w1q)
-                w2q = load_w2(e, hold=False)
+                w2q = load_w2(e)
             else:
-                w2q = load_w2(e, hold=True)
+                w2q = load_w2(e, hold="held_h")
                 hq = first_layer(e, w1q)
                 if e == LAST:
                     shared_second_layer()
                 else:
-                    first_pass = load_w1(e + 1, 0, even)
+                    first_pass = load_w1(e + 1, 0, even, hold="held_y")
             second_layer(e, w2q, hq)
 
-        for h in range(HALVES):
-            result = keep.tile([P, T], F32, name="result%d" % h)
+        for r in range(HALVES):
+            result = keep.tile([P, T], F32, name="result%d" % r)
             for c0, c1 in SPANS:
-                nc.vector.tensor_tensor(result[:, c0:c1], ys[h, c0][:], routed[h][:, c0:c1], ADD)
-                nc.sync.dma_start(out=out[h * P : (h + 1) * P, c0:c1], in_=result[:, c0:c1])
+                nc.vector.tensor_tensor(result[:, c0:c1], ys[r, c0][:], routed[r][:, c0:c1], ADD)
+                nc.sync.dma_start(out=out[r * P : (r + 1) * P, c0:c1], in_=result[:, c0:c1])

from contextlib import ExitStack

import concourse.mybir as mybir
from concourse.masks import make_identity

K, T, E, C, H, N = 1024, 640, 4, 128, 1024, 256
SLOTS = E * C
SHARED = E
LAST = E - 1
FLOPS = 2 * (SLOTS + T) * (K * H + H * N)

F32 = mybir.dt.float32
BF16 = mybir.dt.bfloat16
I32 = mybir.dt.int32
U32 = mybir.dt.uint32
U16 = mybir.dt.uint16
U8 = mybir.dt.uint8
FP8X4 = mybir.dt.float8_e4m3fn_x4
GELU = mybir.ActivationFunctionType.Gelu_apprx_tanh
MULT = mybir.AluOpType.mult
ADD = mybir.AluOpType.add

P = 128
PACK = 4
KP = P * PACK
PASSES = 2
HALVES = N // P
PER_COLUMN = 16
SPANS = ((0, 512), (512, T))
BACKWARDS = (1, 0)


def tile_moe_shr_mlp_gelu_kernel(tc, x_words, x_scales, w1, w2, gate, offs, out):
    nc = tc.nc
    on_scalar, on_vector = nc.scalar.copy, nc.vector.tensor_copy
    even = (on_scalar, on_vector, on_scalar, on_vector)
    all_vector = (on_vector,) * 4
    mostly_vector = (on_scalar, on_vector, on_vector, on_vector)

    with ExitStack() as ctx:
        keep = ctx.enter_context(tc.tile_pool(name="keep", bufs=1))
        raws = ctx.enter_context(tc.tile_pool(name="raws", bufs=7))
        stage = ctx.enter_context(tc.tile_pool(name="stage", bufs=4))
        codes = ctx.enter_context(tc.tile_pool(name="codes", bufs=7))
        two = ctx.enter_context(tc.tile_pool(name="two", bufs=2))
        psum = ctx.enter_context(tc.psum_pool(name="psum", bufs=4))

        offsets = keep.tile([P, SLOTS // PER_COLUMN], U16, name="offsets")
        xw = keep.tile([P, PASSES * T], U32, name="xw", align_bytes=64)
        xs = keep.tile([P, T], U8, name="xs", align_bytes=64)
        gw = keep.tile([P, PASSES * SLOTS], U32, name="gw", align_bytes=64)
        gs = keep.tile([P, SLOTS], U8, name="gs", align_bytes=64)
        gate_sb = keep.tile([P, SLOTS], F32, name="gate_sb")
        routed = [keep.tile([P, T], F32, name="routed%d" % r) for r in range(HALVES)]

        nc.vector.memset(xs[:].bitcast(I32), 0)
        nc.sync.dma_start(
            out=xw[:].bitcast(I32).rearrange("p (o c) -> p o c", o=PASSES),
            in_=x_words.rearrange("o p c j -> p o (c j)").bitcast(I32),
        )
        nc.sync.dma_start(offsets[:], offs)
        for q in range(4):
            nc.sync.dma_start(
                out=xs[32 * q : 32 * q + 4 * PASSES, :].bitcast(I32),
                in_=x_scales[:, 4 * q : 4 * q + 4, :].bitcast(I32),
            )
        for r in range(HALVES):
            nc.vector.memset(routed[r][:], 0.0)
        warm = keep.tile([P, 1], F32, name="warm")
        nc.scalar.activation(warm[:], routed[0][:, 0:1], GELU)
        pair = 2 * C
        for s0 in range(0, SLOTS, pair):
            entries = offsets[:, s0 // PER_COLUMN : (s0 + pair) // PER_COLUMN]
            for o in range(PASSES):
                nc.vector.tensor_copy(
                    gw[:, o * SLOTS + s0 : o * SLOTS + s0 + pair], xw[:, o * T : (o + 1) * T].indirect(entries)
                )
            nc.vector.tensor_copy(gs[:, s0 : s0 + pair], xs[:].indirect(entries))

        def staged(shape, dtype, tag):
            bufs = {"held_h": 1, "held_y": 1, "y": 1, "small": 7}.get(tag, 4)
            return stage.tile(shape, dtype, name=tag, align_bytes=64, bufs=bufs)

        def code_tiles(width, tag, pool):
            words = pool.tile([P, width], U32, name=tag + "_w", align_bytes=64)
            scales = pool.tile([P, width], U8, name=tag + "_s", align_bytes=64)
            return words, scales

        def quantise(rounded, width, tag, pool):
            words, scales = code_tiles(width, tag, pool)
            nc.vector.quantize_mx(out=words[:].bitcast(FP8X4), scales=scales[:], in_=rounded[:])
            return words, scales

        def w1_rows(e, o):
            return w1[e, o * KP : (o + 1) * KP, :].rearrange("(p j) c -> p j c", j=PACK)

        def by_quarter(raw):
            return raw.rearrange("p j (m u v) -> p u m j v", u=2, v=2)

        def load_w1(e, o, copies, hold=None):
            tag, pool = ("w1s%d" % o, two) if e == SHARED else ("w1q", codes)
            raw = raws.tile([P, PACK, H], F32, name="raw")
            nc.sync.dma_start(out=raw[:], in_=w1_rows(e, o))
            rounded = {}
            for g in BACKWARDS:
                rounded[g] = staged([P, PACK * KP], BF16, hold if hold and g == 1 else "w1b")
                dst = rounded[g][:].rearrange("p (u v m j) -> p u m j v", u=2, v=2, j=PACK)
                src = by_quarter(raw[:, :, g * KP : (g + 1) * KP])
                for u in range(2):
                    copies[2 * g + u](dst[:, u], src[:, u])
            return {g: quantise(rounded[g], KP, tag, pool) for g in BACKWARDS}

        def load_last_w1():
            quantised = {}
            for g in BACKWARDS:
                raw = raws.tile([P, PACK, KP], F32, name="raw")
                nc.sync.dma_start(out=raw[:], in_=w1_rows(LAST, 1)[:, :, g * KP : (g + 1) * KP])
                words, scales = code_tiles(KP, "w1q", codes)
                src = by_quarter(raw[:])
                quarters = []
                for u in range(2):
                    rounded = staged([P, 2 * KP], BF16, "small")
                    even[2 * g + u](rounded[:].rearrange("p (v m j) -> p m j v", v=2, j=PACK), src[:, u])
                    quarters.append(rounded)
                for u in range(2):
                    cols = slice(u * 2 * P, (u + 1) * 2 * P)
                    nc.vector.quantize_mx(out=words[:, cols].bitcast(FP8X4), scales=scales[:, cols], in_=quarters[u][:])
                quantised[g] = (words, scales)
            return quantised

        def round_w2(raw, copy, width, tag):
            rounded = staged([P, PACK * width], BF16, tag)
            copy(rounded[:].rearrange("p (c v j) -> p c j v", v=2, j=PACK), raw.rearrange("p j (c v) -> p c j v", v=2))
            return rounded

        def load_w2(e, hold=None):
            raw = raws.tile([P, PASSES, PACK, N], F32, name="raw")
            nc.sync.dma_start(
                out=raw[:].rearrange("p o j n -> p o (j n)"),
                in_=w2[e].rearrange("(o p j) n -> p o (j n)", o=PASSES, j=PACK),
            )
            rounded = {
                1: round_w2(raw[:, 1], on_vector, N, "small"),
                0: round_w2(raw[:, 0], on_scalar, N, hold or "small"),
            }
            return {o: quantise(rounded[o], N, "w2q", codes) for o in BACKWARDS}

        def hidden_block(w1q, g, words, scales, width, c0, hidden, tag):
            bank = psum.tile([P, PACK, C], F32, name=tag)
            for t in range(PACK):
                for o in range(PASSES):
                    w_words, w_scales = w1q[o][g]
                    nc.tensor.matmul_mx(
                        out=bank[:, t, :],
                        lhsT=w_words[:, t * P : (t + 1) * P].bitcast(FP8X4),
                        lhsT_scale=w_scales[:, t * P : (t + 1) * P],
                        rhs=words[:, o * width + c0 : o * width + c0 + C].bitcast(FP8X4),
                        rhs_scale=scales[4 * o : P, c0 : c0 + C],
                        start=(o == 0),
                        stop=(o == PASSES - 1),
                    )
            nc.scalar.activation(hidden.rearrange("p (n t) -> p n t", t=PACK), bank[:].rearrange("p t n -> p n t"), GELU)

        def first_layer(e, w1q):
            hq = {}
            for g in BACKWARDS:
                hidden = staged([P, PACK * C], BF16, "held_h" if g == 0 else "hb")
                hidden_block(w1q, g, gw, gs, SLOTS, e * C, hidden[:], "bank")
                hq[g] = quantise(hidden, C, "hq", codes)
            return hq

        def second_layer(e, w2q, hq):
            bank = psum.tile([P, HALVES, C], F32, name="bank")
            for r in range(HALVES):
                for g in BACKWARDS:
                    nc.tensor.matmul_mx(
                        out=bank[:, r, :],
                        lhsT=w2q[g][0][:, r * P : (r + 1) * P].bitcast(FP8X4),
                        lhsT_scale=w2q[g][1][:, r * P : (r + 1) * P],
                        rhs=hq[g][0][:].bitcast(FP8X4),
                        rhs_scale=hq[g][1][:],
                        start=(g == 1),
                        stop=(g == 0),
                    )
            y = staged([P, HALVES, C], F32, "y" if e == LAST - 1 else "held_y")
            (on_vector if e == LAST else on_scalar)(y[:], bank[:])
            entries = offsets[:, e * C // PER_COLUMN : (e + 1) * C // PER_COLUMN]
            for r in range(HALVES):
                nc.vector.tensor_tensor(routed[r][:].indirect(entries), y[:, r, :], gate_sb[:, e * C : (e + 1) * C], MULT)

        hs_w = [keep.tile([P, T], U32, name="hs_w%d" % g, align_bytes=64) for g in range(PASSES)]
        hs_s = [keep.tile([P, T], U8, name="hs_s%d" % g, align_bytes=64) for g in range(PASSES)]

        def shared_first_layer(g, w1q):
            hidden = keep.tile([P, PACK * T], BF16, name="hsb%d" % g, align_bytes=64)
            for c0 in range(0, T, C):
                hidden_block(w1q, g, xw, xs, T, c0, hidden[:, PACK * c0 : PACK * (c0 + C)], "bank_s")
            for c0, c1 in SPANS:
                nc.vector.quantize_mx(
                    out=hs_w[g][:, c0:c1].bitcast(FP8X4), scales=hs_s[g][:, c0:c1], in_=hidden[:, PACK * c0 : PACK * c1]
                )

        ys = {}

        def shared_pass(g, r, w_words, w_scales):
            for c0, c1 in SPANS:
                if g == 0:
                    ys[r, c0] = psum.tile([P, c1 - c0], F32, name="bank_s")
                nc.tensor.matmul_mx(
                    out=ys[r, c0][:],
                    lhsT=w_words.bitcast(FP8X4),
                    lhsT_scale=w_scales,
                    rhs=hs_w[g][:, c0:c1].bitcast(FP8X4),
                    rhs_scale=hs_s[g][:, c0:c1],
                    start=(g == 0),
                    stop=(g == PASSES - 1),
                )

        def load_shared_w2(g):
            raw = raws.tile([P, PACK, N], F32, name="raw")
            nc.sync.dma_start(out=raw[:], in_=w2[SHARED, g * KP : (g + 1) * KP, :].rearrange("(p j) n -> p j n", j=PACK))
            return raw

        def shared_second_layer():
            words, scales = quantise(round_w2(load_shared_w2(0)[:], on_vector, N, "small"), N, "w2q", codes)
            for r in range(HALVES):
                shared_pass(0, r, words[:, r * P : (r + 1) * P], scales[:, r * P : (r + 1) * P])
            raw = load_shared_w2(1)
            rounded = [
                round_w2(raw[:, :, r * P : (r + 1) * P], on_scalar, P, "held_y" if r == 1 else "small")
                for r in range(HALVES)
            ]
            for r in range(HALVES):
                words, scales = quantise(rounded[r], P, "w2q", codes)
                shared_pass(1, r, words[:], scales[:])

        def spread_gate():
            identity = keep.tile([P, P], F32, name="identity")
            make_identity(nc, identity[:])
            rows = keep.tile([P, C], F32, name="gate_rows")
            nc.vector.memset(rows[:], 0.0)
            nc.sync.dma_start(out=rows[0:E, :], in_=gate[0, :].rearrange("(e c) -> e c", e=E))
            turned = psum.tile([P, P], F32, name="bank")
            nc.tensor.transpose(turned[:], rows[:], identity[:])
            columns = keep.tile([P, E], F32, name="gate_columns")
            nc.scalar.copy(columns[:], turned[:, 0:E])
            spread = psum.tile([P, E, C], F32, name="bank")
            for e in range(E):
                nc.tensor.transpose(spread[:, e, :], columns[:, e : e + 1].to_broadcast([P, P]), identity[:])
            nc.scalar.copy(gate_sb[:].rearrange("p (e c) -> p e c", e=E), spread[:])

        spread_gate()
        shared_w1q = [load_w1(SHARED, o, even) for o in range(PASSES)]
        first_pass = load_w1(0, 0, all_vector)
        for g in range(PASSES):
            shared_first_layer(g, shared_w1q)

        for e in range(E):
            if e == LAST:
                w1q = [first_pass, load_last_w1()]
            else:
                w1q = [first_pass, load_w1(e, 1, mostly_vector if e == 0 else even)]
            if e == LAST - 1:
                first_pass = load_w1(LAST, 0, even, hold="held_h")
                hq = first_layer(e, w1q)
                w2q = load_w2(e)
            else:
                w2q = load_w2(e, hold="held_h")
                hq = first_layer(e, w1q)
                if e == LAST:
                    shared_second_layer()
                else:
                    first_pass = load_w1(e + 1, 0, even, hold="held_y")
            second_layer(e, w2q, hq)

        for r in range(HALVES):
            result = keep.tile([P, T], F32, name="result%d" % r)
            for c0, c1 in SPANS:
                nc.vector.tensor_tensor(result[:, c0:c1], ys[r, c0][:], routed[r][:, c0:c1], ADD)
                nc.sync.dma_start(out=out[r * P : (r + 1) * P, c0:c1], in_=result[:, c0:c1])
